import numpy as np
import ml_dtypes


def mxq(x, axis, fmt="e4m3"):
    dtype, down = {"e4m3": (ml_dtypes.float8_e4m3fn, 7), "e5m2": (ml_dtypes.float8_e5m2, 14)}[fmt]
    v = np.moveaxis(np.asarray(x, np.float32).astype(ml_dtypes.bfloat16).astype(np.float64), axis, -1)
    blocks = v.reshape(v.shape[:-1] + (-1, 32))
    amax = np.abs(blocks).max(-1, keepdims=True)
    byte = np.maximum(np.where(amax > 0, np.frexp(amax)[1] - 1 + 127, 0) - down, 1)
    scale = np.exp2(byte - 127.0)
    codes = (blocks / scale).astype(np.float32).astype(dtype).astype(np.float64)
    return np.moveaxis((codes * scale).reshape(v.shape), -1, axis)


WIDE = False


def mx_kscale(k):
    if not WIDE:
        return np.ones(k)
    levels = np.array([10, -10, 5, -5, 0])
    if k % 512:
        return np.exp2(np.random.permutation(np.resize(levels, k // 32))).repeat(32)
    a = np.empty((k // 512, 16))
    for p in range(k // 512):
        a[p, :8] = np.random.permutation(np.resize(levels, 8))
        for g in range(8):
            far = levels[np.abs(levels - a[p, g]) >= 10]
            a[p, g + 8] = far[np.random.randint(len(far))]
    return np.exp2(a.ravel()).repeat(32)


def f64(x):
    return np.asarray(x).astype(np.float64)


def striped(idx):
    return np.tile(idx.reshape(-1, 16).T, (8, 1)).astype(np.uint16)


def unstriped(offs):
    return offs[:16].T.reshape(-1).astype(np.int64)


E2M1 = np.array([0.0, 0.5, 1.0, 1.5, 2.0, 3.0, 4.0, 6.0, -0.0, -0.5, -1.0, -1.5, -2.0, -3.0, -4.0, -6.0])


def pack_weight(w, fmt):
    k, n = w.shape
    w = f64(np.asarray(w, np.float32).astype(ml_dtypes.bfloat16)).reshape(k // 32, 32, n)
    amax = np.abs(w).max(1)
    if fmt == "e4m3":
        byte = np.frexp(amax)[1] - 1 + 127 - 7
    else:
        mant, ex = np.frexp(amax / 6.0)
        byte = np.where(mant > 0.5, ex, ex - 1) + 127
    byte = np.clip(np.where(amax > 0, byte, 1), 1, 254)
    scaled = (w * np.exp2(127.0 - byte)[:, None, :]).reshape(k, n).astype(np.float32)
    by_word = np.ascontiguousarray(scaled.reshape(k // 512, 128, 4, n).transpose(0, 1, 3, 2))
    if fmt == "e4m3":
        words = by_word.astype(ml_dtypes.float8_e4m3fn).view(np.uint8)
    else:
        c = by_word.astype(ml_dtypes.float4_e2m1fn).view(np.uint8) & 0xF
        words = (c[..., 0::2] | (c[..., 1::2] << 4)).reshape(k // 512, 128, 2 * n)
    return np.ascontiguousarray(words), np.ascontiguousarray(byte.astype(np.uint8).reshape(k // 512, 16, n))


def unpack_weight(words, scales, fmt):
    g, _, n = scales.shape
    words = np.ascontiguousarray(words).reshape(g, 128, n, -1)
    if fmt == "e4m3":
        vals = words.view(ml_dtypes.float8_e4m3fn).astype(np.float64)
    else:
        nib = np.empty((g, 128, n, 4), np.uint8)
        nib[..., 0::2] = words & 0xF
        nib[..., 1::2] = words >> 4
        vals = E2M1[nib]
    vals = vals * np.repeat(np.exp2(scales.astype(np.float64) - 127.0), 8, axis=1)[..., None]
    return vals.transpose(0, 1, 3, 2).reshape(g * 512, n)


def gelu(v):
    return 0.5 * v * (1.0 + np.tanh(np.sqrt(2.0 / np.pi) * (v + 0.044715 * v**3)))


def bf(x):
    return np.asarray(x, np.float32).astype(ml_dtypes.bfloat16)


def planes(Y):
    n, m = Y.shape
    b = f64(bf(Y)).reshape(n // 32, 32, m)
    amax = np.abs(b).max(1)
    byte = np.clip(np.where(amax > 0, np.frexp(amax)[1] - 1 + 127 - 7, 1), 1, 254)
    codes = (b * np.exp2(127.0 - byte)[:, None, :]).reshape(n, m).astype(np.float32).astype(ml_dtypes.float8_e4m3fn).view(np.uint8)
    words = codes.reshape(n // 512, 128, 4, m).transpose(0, 1, 3, 2)
    return np.ascontiguousarray(words), np.ascontiguousarray(byte.astype(np.uint8).reshape(n // 512, 16, m))


K, T, S, H, T2, P, N = 1024, 4096, 1024, 1024, 2048, 1024, 384

def setup_inputs():
    n = np.random.standard_normal
    s = mx_kscale(K)[:, None]
    u = mx_kscale(H)[:, None]
    d = {}
    d["tab_words"], d["tab_scales"] = pack_weight(n((K, T)) * s, "e4m3")
    d["offs"] = striped(np.random.permutation(T)[:S])
    d["w1"] = (n((K, H)) / K**0.5 / s * u.T).astype(np.float32)
    d["tide"] = (n((H, S)) * u).astype(np.float32)
    d["page0"] = (n((H, T2)) * u).astype(np.float32)
    d["wgs"] = np.exp(0.3 * n((128, S))).astype(np.float32)
    d["offs2"] = striped(np.random.permutation(T2)[:S])
    d["offs3"] = striped(np.random.permutation(T2)[:P])
    d["w2_words"], d["w2_scales"] = pack_weight(n((H, N)) / H**0.5 / u, "e2m1")
    d["w3"] = (n((H, N)) / H**0.5 / u).astype(np.float32)
    return d

def reference(tab_words, tab_scales, offs, w1, tide, page0, wgs, offs2, offs3, w2_words, w2_scales, w3):
    v = unpack_weight(tab_words, tab_scales, "e4m3")[:, unstriped(offs)]
    a = mxq(f64(w1), 0, "e4m3").T @ v
    h = np.maximum(a, f64(tide))
    page = f64(page0).copy()
    page[:, unstriped(offs2)] = np.tile(f64(wgs), (H // 128, 1)) * h
    x = mxq(np.abs(page[:, unstriped(offs3)]), 0, "e4m3")
    y1 = unpack_weight(w2_words, w2_scales, "e2m1").T @ x
    y2 = mxq(f64(w3), 0, "e4m3").T @ x
    y = np.sqrt(np.square(y1) + np.square(y2))
    words, scales = planes(page)
    return y, page, words, scales

@@ -1,0 +1,292 @@
+from contextlib import ExitStack
+
+import concourse.mybir as mybir
+
+K, T, S, H, T2, PICK, N = 1024, 4096, 1024, 1024, 2048, 1024, 384
+FLOPS = 2 * K * H * S + 2 * 2 * H * N * PICK
+
+F32 = mybir.dt.float32
+BF16 = mybir.dt.bfloat16
+I32 = mybir.dt.int32
+U32 = mybir.dt.uint32
+U16 = mybir.dt.uint16
+U8 = mybir.dt.uint8
+FP8X4 = mybir.dt.float8_e4m3fn_x4
+FP4X4 = mybir.dt.float4_e2m1fn_x4
+ALU = mybir.AluOpType
+ACT = mybir.ActivationFunctionType
+
+P = 128
+PACK = 4
+PASS = P * PACK
+HALF = 512
+QUARTER = 256
+LANES = 16
+TILES = H // P
+N_TILES = N // P
+HELD = (2, 4, 5, 6)
+
+
+def tile_list_nest_board_risk_kernel(tc, tab_words, tab_scales, offs, w1, tide, page0, wgs, offs2, offs3,
+                                              w2_words, w2_scales, w3, out_0, out_1, out_2, out_3):
+    nc = tc.nc
+    tide_rows = tide.rearrange("(b p t) j -> b t p j", p=P, t=PACK)
+    page_rows = page0.rearrange("(b p t) m -> b t p m", p=P, t=PACK)
+    out_rows = out_1.rearrange("(b p t) m -> b t p m", p=P, t=PACK)
+    wgs_rows = wgs.rearrange("(i t) j -> i t j", t=PACK)
+    y_rows = out_0.rearrange("(u p) m -> p u m", p=P)
+
+    with ExitStack() as ctx:
+        sb = ctx.enter_context(tc.tile_pool(name="sb", bufs=1))
+        ps = ctx.enter_context(tc.psum_pool(name="ps", bufs=4))
+
+        idx = sb.tile([P, S // LANES], U16, name="idx")
+        idx2 = sb.tile([P, S // LANES], U16, name="idx2")
+        idx3 = sb.tile([P, PICK // LANES], U16, name="idx3")
+        tab_s = sb.tile([P, T], U8, name="tab_s", align_bytes=64)
+        v_codes = sb.tile([P, 2, S], U32, name="v_codes", align_bytes=64)
+        v_scales = sb.tile([P, S], U8, name="v_scales", align_bytes=64)
+        w1_codes = {0: sb.tile([P, 2, PASS], U32, name="w1_codes0", align_bytes=64)}
+        w1_scales = sb.tile([P, 2, 2, PASS], U8, name="w1_scales", align_bytes=64)
+        w2_codes = sb.tile([P, 2, 2 * N], U8, name="w2_codes", align_bytes=64)
+        w2_plane = sb.tile([P, 2, N], U8, name="w2_plane", align_bytes=64)
+        w3_scales = sb.tile([P, 2, N], U8, name="w3_scales", align_bytes=64)
+        x_codes = {1: sb.tile([P, PICK], U32, name="x_codes1", align_bytes=64)}
+        x_scales = sb.tile([P, 2, PICK], U8, name="x_scales", align_bytes=64)
+        x_round = sb.tile([P, PICK, PACK], BF16, name="x_round", align_bytes=64)
+        gain_first = [sb.tile([P, HALF], F32, name="gain_first%d" % u) for u in range(2)]
+        gain_rest = sb.tile([P, PACK - 1, S], F32, name="gain_rest")
+
+        def big(shape, dtype, name):
+            return sb.tile(shape, dtype, name=name, tag="big", bufs=2, align_bytes=64)
+
+        def entries(lst, lo, hi):
+            return lst[:, lo // LANES: hi // LANES]
+
+        def load_weight(rows, name):
+            raw = sb.tile([P, PACK, rows.shape[1]], F32, name=name, tag="raw", bufs=2)
+            nc.sync.dma_start(out=raw[:], in_=rows.rearrange("(p j) c -> p j c", j=PACK))
+            return raw
+
+        def copy_on(engine, out, in_):
+            if engine == "vector":
+                nc.vector.tensor_copy(out=out, in_=in_)
+            else:
+                nc.scalar.copy(out=out, in_=in_)
+
+        def after(i, shape, dtype, name):
+            return sb.tile(shape, dtype, name=name, tag="after%d" % i, align_bytes=64)
+
+        def new_h(i):
+            if i in HELD:
+                return after(i, [P, S], F32, "h%d" % i)
+            return sb.tile([P, S], F32, name="h%d" % i, tag="h", bufs=2)
+
+        def round_w1(raw, b, a, engine):
+            rounded = sb.tile([P, PACK * PASS], BF16, name="w1_round%d%d" % (b, a), tag="round", bufs=2, align_bytes=64)
+            copy_on(engine, rounded[:].rearrange("p (t m j) -> p m j t", t=PACK, j=PACK),
+                    raw[:].rearrange("p j (m t) -> p m j t", t=PACK))
+            return rounded
+
+        def quantise_w1(rounded, b, a):
+            nc.vector.quantize_mx(out=w1_codes[b][:, a, :].bitcast(FP8X4), scales=w1_scales[:, b, a, :], in_=rounded[:])
+
+        def round_w3(raw, a):
+            rounded = sb.tile([P, PACK * N], BF16, name="w3_round%d" % a, tag="round", bufs=2, align_bytes=64)
+            nc.scalar.copy(out=rounded[:].rearrange("p (c i j) -> p c j i", i=4, j=PACK),
+                           in_=raw[:].rearrange("p j (c i) -> p c j i", i=4))
+            return rounded
+
+        def load_page(i):
+            page = sb.tile([P, T2], F32, name="page%d" % i, tag="page", bufs=4)
+            nc.sync.dma_start(out=page[:], in_=page_rows[i // PACK, i % PACK])
+            return page
+
+        def load_tide(i):
+            floor = sb.tile([P, S], F32, name="floor%d" % i, tag="floor", bufs=3)
+            nc.sync.dma_start(out=floor[:], in_=tide_rows[i // PACK, i % PACK])
+            return floor
+
+        def load_gain_first(u):
+            for q in range(4):
+                nc.sync.dma_start(out=gain_first[u][32 * q: 32 * q + 32, :], in_=wgs_rows[:, 0, u * HALF:(u + 1) * HALF])
+
+        def features(i, u, floor_half, h):
+            b, t = divmod(i, PACK)
+            cols = slice(u * HALF, (u + 1) * HALF)
+            rows = slice(t * P, (t + 1) * P)
+            acc = ps.tile([P, HALF], F32, name="acc%d%d" % (i, u), tag="acc")
+            for a in range(2):
+                nc.tensor.matmul_mx(out=acc[:], lhsT=w1_codes[b][:, a, rows].bitcast(FP8X4), lhsT_scale=w1_scales[:, b, a, rows],
+                                    rhs=v_codes[:, a, cols].bitcast(FP8X4), rhs_scale=v_scales[4 * a:P, cols],
+                                    start=(a == 0), stop=(a == 1))
+            nc.vector.tensor_tensor(out=h[:, cols], in0=acc[:], in1=floor_half, op=ALU.max)
+
+        def put(page, h, gain, lo, hi):
+            nc.vector.tensor_tensor(out=page[:].indirect(entries(idx2, lo, hi)), in0=h[:, lo:hi], in1=gain, op=ALU.mult)
+
+        def put_tile(i, page, h):
+            t = i % PACK
+            if t == 0:
+                for u in range(2):
+                    put(page, h, gain_first[u][:], u * HALF, (u + 1) * HALF)
+            else:
+                put(page, h, gain_rest[:, t - 1, :], 0, S)
+
+        def fetch(page, picked, e, lo, hi):
+            nc.vector.tensor_copy(out=picked[:, e, lo:hi], in_=page[:].indirect(entries(idx3, lo, hi)))
+
+        def round_x(picked, pair, lo, hi):
+            nc.scalar.activation(out=x_round[:, lo:hi, 2 * pair:2 * pair + 2],
+                                 in_=picked[:, :, lo:hi].rearrange("p e m -> p m e"), func=ACT.Abs)
+
+        def quantise_x(b, lo, hi):
+            nc.vector.quantize_mx(out=x_codes[b][:, lo:hi].bitcast(FP8X4), scales=x_scales[:, b, lo:hi],
+                                  in_=x_round[:, lo:hi, :].rearrange("p m t -> p (m t)"))
+
+        def quantise_page(woven, codes, scales, lo, hi):
+            nc.vector.quantize_mx(out=codes[:, lo:hi].bitcast(FP8X4), scales=scales[:, lo:hi],
+                                  in_=woven[:, lo:hi, :].rearrange("p m t -> p (m t)"))
+
+        def store_codes(b, codes, lo, hi):
+            words = out_2[b].rearrange("p m t -> p (m t)").bitcast(I32)
+            nc.sync.dma_start(out=words[:, lo:hi], in_=codes[:, lo:hi].bitcast(I32))
+
+        def store_scales(b, scales):
+            for q in range(4):
+                nc.sync.dma_start(out=out_3[b, 4 * q:4 * q + 4, :].bitcast(I32), in_=scales[32 * q:32 * q + 4, :].bitcast(I32))
+
+        def score(q, w3_codes):
+            cols = slice(q * QUARTER, (q + 1) * QUARTER)
+            squares = sb.tile([P, N_TILES, 2, QUARTER], F32, name="squares%d" % q, tag="raw", bufs=2)
+            for u in range(N_TILES):
+                pair = ps.tile([P, 2, QUARTER], F32, name="pair%d%d" % (q, u), tag="pair")
+                rows = slice(u * P, (u + 1) * P)
+                for b in range(2):
+                    nc.tensor.matmul_mx(out=pair[:, 0, :], lhsT=w2_codes[:, b, 2 * u * P:2 * (u + 1) * P].bitcast(FP4X4),
+                                        lhsT_scale=w2_plane[:, b, rows], rhs=x_codes[b][:, cols].bitcast(FP8X4),
+                                        rhs_scale=x_scales[:, b, cols], start=(b == 0), stop=False)
+                    nc.tensor.matmul_mx(out=pair[:, 1, :], lhsT=w3_codes[:, b, rows].bitcast(FP8X4),
+                                        lhsT_scale=w3_scales[:, b, rows], rhs=x_codes[b][:, cols].bitcast(FP8X4),
+                                        rhs_scale=x_scales[:, b, cols], start=False, stop=(b == 1))
+                nc.scalar.activation(out=squares[:, u], in_=pair[:], func=ACT.Square)
+            total = sb.tile([P, N_TILES, QUARTER], F32, name="total%d" % q, tag="round", bufs=2, align_bytes=64)
+            nc.vector.tensor_tensor(out=total[:], in0=squares[:, :, 0, :], in1=squares[:, :, 1, :], op=ALU.add)
+            nc.scalar.activation(out=total[:], in_=total[:], func=ACT.Sqrt)
+            nc.sync.dma_start(out=y_rows[:, :, cols], in_=total[:])
+
+        nc.vector.memset(tab_s[:].bitcast(I32), 0)
+        nc.vector.memset(w2_plane[:].rearrange("p b c -> p (b c)").bitcast(I32), 0)
+
+        nc.sync.dma_start(out=idx[:], in_=offs)
+        tab_w = [big([P, T], I32, "tab_w%d" % a) for a in range(2)]
+        nc.sync.dma_start(out=tab_w[0][:], in_=tab_words[0].rearrange("p n t -> p (n t)").bitcast(I32))
+        for q in range(4):
+            nc.sync.dma_start(out=tab_s[32 * q:32 * q + 8, :].bitcast(I32), in_=tab_scales[:, 4 * q:4 * q + 4, :].bitcast(I32))
+        raw = [load_weight(w1[a * PASS:(a + 1) * PASS, 0:PASS], "w1_raw0%d" % a) for a in range(2)]
+        nc.sync.dma_start(out=tab_w[1][:], in_=tab_words[1].rearrange("p n t -> p (n t)").bitcast(I32))
+        floor_first = [sb.tile([P, HALF], F32, name="floor_first%d" % u, tag="floor", bufs=3) for u in range(2)]
+        nc.sync.dma_start(out=floor_first[0][:], in_=tide_rows[0, 0][:, 0:HALF])
+        nc.sync.dma_start(out=idx2[:], in_=offs2)
+        load_gain_first(0)
+        pages = {0: load_page(0)}
+        nc.sync.dma_start(out=floor_first[1][:], in_=tide_rows[0, 0][:, HALF:S])
+        load_gain_first(1)
+        nc.sync.dma_start(out=idx3[:], in_=offs3)
+        floors = {1: load_tide(1)}
+        for q in range(4):
+            nc.sync.dma_start(out=gain_rest[32 * q:32 * q + 32], in_=wgs_rows[:, 1:PACK, :])
+        pages[1] = load_page(1)
+
+        nc.vector.tensor_copy(out=v_codes[:, 0, :], in_=tab_w[0][:].bitcast(U32).indirect(idx[:]))
+        nc.vector.tensor_copy(out=v_scales[:], in_=tab_s[:].indirect(idx[:]))
+        quantise_w1(round_w1(raw[0], 0, 0, "scalar"), 0, 0)
+        quantise_w1(round_w1(raw[1], 0, 1, "vector"), 0, 1)
+        for u in range(2):
+            nc.vector.tensor_copy(out=v_codes[:, 1, u * HALF:(u + 1) * HALF],
+                                  in_=tab_w[1][:].bitcast(U32).indirect(entries(idx, u * HALF, (u + 1) * HALF)))
+
+        h = new_h(0)
+        for u in range(2):
+            features(0, u, floor_first[u][:], h)
+            put(pages[0], h, gain_first[u][:], u * HALF, (u + 1) * HALF)
+
+        raw = [load_weight(w1[a * PASS:(a + 1) * PASS, PASS:2 * PASS], "w1_raw1%d" % a) for a in range(2)]
+        w1_round = [round_w1(raw[a], 1, a, "scalar") for a in range(2)]
+
+        last = TILES - 1
+        picked = pairs = woven = woven_last = planes = w3_round = w3_codes = None
+        for i in range(TILES):
+            b, t = divmod(i, PACK)
+            pair, e = divmod(t, 2)
+            if i + 2 < TILES:
+                floors[i + 2] = load_tide(i + 2)
+                pages[i + 2] = load_page(i + 2)
+            nc.sync.dma_start(out=out_rows[b, t], in_=pages[i][:])
+            if i == last:
+                break
+            if e == 0:
+                picked = sb.tile([P, 2, PICK], F32, name="picked%d" % i, tag="picked", bufs=2)
+            if i == 0:
+                pairs = big([P, 2, T2, 2], BF16, "pairs")
+            if i == 4:
+                woven_last = big([P, T2, PACK], BF16, "woven1")
+            if i == 6:
+                planes = big([P, 2, T2], BF16, "planes")
+            if b == 0:
+                nc.scalar.copy(out=pairs[:, pair, :, e], in_=pages[i][:])
+            elif pair == 0:
+                nc.scalar.copy(out=woven_last[:, :, t], in_=pages[i][:])
+            else:
+                nc.scalar.copy(out=planes[:, 0, :], in_=pages[i][:])
+            if i == 2:
+                w1_codes[1] = after(2, [P, 2, PASS], U32, "w1_codes1")
+                for a in range(2):
+                    quantise_w1(w1_round[a], 1, a)
+                nc.sync.dma_start(out=w2_codes[:].bitcast(I32), in_=w2_words.rearrange("b p c -> p b c").bitcast(I32))
+                for q in range(4):
+                    nc.sync.dma_start(out=w2_plane[32 * q:32 * q + 4].bitcast(I32),
+                                      in_=w2_scales[:, 4 * q:4 * q + 4, :].rearrange("b r c -> r b c").bitcast(I32))
+                w3_round = [round_w3(load_weight(w3[a * PASS:(a + 1) * PASS, :], "w3_raw%d" % a), a) for a in range(2)]
+            h = new_h(i + 1)
+            for u in range(2):
+                features(i + 1, u, floors[i + 1][:, u * HALF:(u + 1) * HALF], h)
+            fetch(pages[i], picked, e, 0, PICK)
+            if e == 1:
+                round_x(picked, pair, 0, PICK)
+            if i == 3:
+                woven = big([P, T2, PACK], BF16, "woven0")
+                nc.scalar.copy(out=woven[:].rearrange("p m t -> p (m t)").bitcast(U32).rearrange("p (m h) -> p m h", h=2),
+                               in_=pairs[:].rearrange("p h m e -> p (h m e)").bitcast(U32).rearrange("p (h m) -> p m h", h=2))
+            if i == 4:
+                x_codes[0] = after(4, [P, PICK], U32, "x_codes0")
+                quantise_x(0, 0, PICK)
+            if i == 5:
+                codes = after(5, [P, T2], U32, "codes0")
+                scales = sb.tile([P, T2], U8, name="scales0", align_bytes=64)
+                for u in range(2):
+                    quantise_page(woven, codes, scales, u * T2 // 2, (u + 1) * T2 // 2)
+                store_codes(0, codes, 0, T2)
+                store_scales(0, scales)
+            if i == 6:
+                w3_codes = after(6, [P, 2, N], U32, "w3_codes")
+                for a in range(2):
+                    nc.vector.quantize_mx(out=w3_codes[:, a, :].bitcast(FP8X4), scales=w3_scales[:, a, :], in_=w3_round[a][:])
+            put_tile(i + 1, pages[i + 1], h)
+
+        codes = sb.tile([P, T2], U32, name="codes1", align_bytes=64)
+        scales = sb.tile([P, T2], U8, name="scales1", align_bytes=64)
+        for q in range(4):
+            fetch(pages[last], picked, 1, q * QUARTER, (q + 1) * QUARTER)
+            round_x(picked, 1, q * QUARTER, (q + 1) * QUARTER)
+        for q in range(4):
+            quantise_x(1, q * QUARTER, (q + 1) * QUARTER)
+        for q in range(4):
+            lo, hi = q * HALF, (q + 1) * HALF
+            score(q, w3_codes)
+            nc.vector.tensor_copy(out=planes[:, 1, lo:hi], in_=pages[last][:, lo:hi])
+            nc.vector.tensor_copy(out=woven_last[:, lo:hi, 2:4], in_=planes[:, :, lo:hi].rearrange("p e m -> p m e"))
+            quantise_page(woven_last, codes, scales, lo, hi)
+            if q % 2 == 1:
+                store_codes(1, codes, lo - HALF, hi)
+        store_scales(1, scales)

@@ -1,6 +1,7 @@
 from contextlib import ExitStack
 
 import concourse.mybir as mybir
+from concourse.masks import make_identity
 
 K, T, S, H, T2, PICK, N = 1024, 4096, 1024, 1024, 2048, 1024, 384
 FLOPS = 2 * K * H * S + 2 * 2 * H * N * PICK
@@ -33,18 +34,17 @@ def tile_list_nest_board_risk_kernel(tc, tab_words, tab_scales, offs, w1, tide, 
     tide_rows = tide.rearrange("(b p t) j -> b t p j", p=P, t=PACK)
     page_rows = page0.rearrange("(b p t) m -> b t p m", p=P, t=PACK)
     out_rows = out_1.rearrange("(b p t) m -> b t p m", p=P, t=PACK)
-    wgs_rows = wgs.rearrange("(i t) j -> i t j", t=PACK)
     y_rows = out_0.rearrange("(u p) m -> p u m", p=P)
 
     with ExitStack() as ctx:
         sb = ctx.enter_context(tc.tile_pool(name="sb", bufs=1))
-        ps = ctx.enter_context(tc.psum_pool(name="ps", bufs=4))
+        ps = ctx.enter_context(tc.psum_pool(name="ps", bufs=8))
 
         idx = sb.tile([P, S // LANES], U16, name="idx")
         idx2 = sb.tile([P, S // LANES], U16, name="idx2")
         idx3 = sb.tile([P, PICK // LANES], U16, name="idx3")
-        tab_s = sb.tile([P, T], U8, name="tab_s", align_bytes=64)
-        v_codes = sb.tile([P, 2, S], U32, name="v_codes", align_bytes=64)
+        tab_s = sb.tile([P, T], U8, name="tab_s", tag="tab_s", align_bytes=64)
+        v_codes = [sb.tile([P, S], U32, name="v_codes0", align_bytes=64)]
         v_scales = sb.tile([P, S], U8, name="v_scales", align_bytes=64)
         w1_codes = {0: sb.tile([P, 2, PASS], U32, name="w1_codes0", align_bytes=64)}
         w1_scales = sb.tile([P, 2, 2, PASS], U8, name="w1_scales", align_bytes=64)
@@ -54,8 +54,8 @@ def tile_list_nest_board_risk_kernel(tc, tab_words, tab_scales, offs, w1, tide, 
         x_codes = {1: sb.tile([P, PICK], U32, name="x_codes1", align_bytes=64)}
         x_scales = sb.tile([P, 2, PICK], U8, name="x_scales", align_bytes=64)
         x_round = sb.tile([P, PICK, PACK], BF16, name="x_round", align_bytes=64)
-        gain_first = [sb.tile([P, HALF], F32, name="gain_first%d" % u) for u in range(2)]
-        gain_rest = sb.tile([P, PACK - 1, S], F32, name="gain_rest")
+        gain = sb.tile([P, PACK, S], F32, name="gain")
+        ident = sb.tile([P, P], F32, name="ident")
 
         def big(shape, dtype, name):
             return sb.tile(shape, dtype, name=name, tag="big", bufs=2, align_bytes=64)
@@ -107,31 +107,39 @@ def tile_list_nest_board_risk_kernel(tc, tab_words, tab_scales, offs, w1, tide, 
             nc.sync.dma_start(out=floor[:], in_=tide_rows[i // PACK, i % PACK])
             return floor
 
-        def load_gain_first(u):
-            for q in range(4):
-                nc.sync.dma_start(out=gain_first[u][32 * q: 32 * q + 32, :], in_=wgs_rows[:, 0, u * HALF:(u + 1) * HALF])
+        def bank(name):
+            return ps.tile([P, HALF], F32, name=name, tag="bank")
+
+        def turn_gain(rows, u):
+            turned = bank("turned%d" % u)
+            for c in range(4):
+                col = u * HALF + c * P
+                nc.tensor.transpose(turned[:, c * P:(c + 1) * P], rows[:, col:col + P], ident[:])
+            dealt = sb.tile([P, 4, PACK, 4, 32], F32, name="dealt%d" % u, tag="picked", bufs=2)
+            nc.scalar.copy(out=dealt[:], in_=turned[:].rearrange("p (c i t) -> p c t i", c=4, t=PACK).unsqueeze(3)
+                           .broadcast_to([P, 4, PACK, 4, 32]))
+            return dealt
+
+        def deal_gain(dealt, t, u):
+            back = bank("back%d%d" % (t, u))
+            for c in range(4):
+                nc.tensor.transpose(back[:, c * P:(c + 1) * P], dealt[:, c, t].rearrange("p q i -> p (q i)"), ident[:])
+            nc.scalar.copy(out=gain[:, t, u * HALF:(u + 1) * HALF], in_=back[:])
 
         def features(i, u, floor_half, h):
             b, t = divmod(i, PACK)
             cols = slice(u * HALF, (u + 1) * HALF)
             rows = slice(t * P, (t + 1) * P)
-            acc = ps.tile([P, HALF], F32, name="acc%d%d" % (i, u), tag="acc")
+            acc = bank("acc%d%d" % (i, u))
             for a in range(2):
                 nc.tensor.matmul_mx(out=acc[:], lhsT=w1_codes[b][:, a, rows].bitcast(FP8X4), lhsT_scale=w1_scales[:, b, a, rows],
-                                    rhs=v_codes[:, a, cols].bitcast(FP8X4), rhs_scale=v_scales[4 * a:P, cols],
+                                    rhs=v_codes[a][:, cols].bitcast(FP8X4), rhs_scale=v_scales[4 * a:P, cols],
                                     start=(a == 0), stop=(a == 1))
             nc.vector.tensor_tensor(out=h[:, cols], in0=acc[:], in1=floor_half, op=ALU.max)
 
-        def put(page, h, gain, lo, hi):
-            nc.vector.tensor_tensor(out=page[:].indirect(entries(idx2, lo, hi)), in0=h[:, lo:hi], in1=gain, op=ALU.mult)
-
-        def put_tile(i, page, h):
-            t = i % PACK
-            if t == 0:
-                for u in range(2):
-                    put(page, h, gain_first[u][:], u * HALF, (u + 1) * HALF)
-            else:
-                put(page, h, gain_rest[:, t - 1, :], 0, S)
+        def put(i, page, h, lo, hi):
+            nc.vector.tensor_tensor(out=page[:].indirect(entries(idx2, lo, hi)), in0=h[:, lo:hi],
+                                    in1=gain[:, i % PACK, lo:hi], op=ALU.mult)
 
         def fetch(page, picked, e, lo, hi):
             nc.vector.tensor_copy(out=picked[:, e, lo:hi], in_=page[:].indirect(entries(idx3, lo, hi)))
@@ -156,63 +164,71 @@ def tile_list_nest_board_risk_kernel(tc, tab_words, tab_scales, offs, w1, tide, 
             for q in range(4):
                 nc.sync.dma_start(out=out_3[b, 4 * q:4 * q + 4, :].bitcast(I32), in_=scales[32 * q:32 * q + 4, :].bitcast(I32))
 
-        def score(q, w3_codes):
+        def score(q, w3_codes, steps):
             cols = slice(q * QUARTER, (q + 1) * QUARTER)
             squares = sb.tile([P, N_TILES, 2, QUARTER], F32, name="squares%d" % q, tag="raw", bufs=2)
+            total = sb.tile([P, N_TILES, QUARTER], F32, name="total%d" % q, tag="round", bufs=2, align_bytes=64)
             for u in range(N_TILES):
-                pair = ps.tile([P, 2, QUARTER], F32, name="pair%d%d" % (q, u), tag="pair")
+                both = bank("both%d%d" % (q, u))
                 rows = slice(u * P, (u + 1) * P)
                 for b in range(2):
-                    nc.tensor.matmul_mx(out=pair[:, 0, :], lhsT=w2_codes[:, b, 2 * u * P:2 * (u + 1) * P].bitcast(FP4X4),
-                                        lhsT_scale=w2_plane[:, b, rows], rhs=x_codes[b][:, cols].bitcast(FP8X4),
-                                        rhs_scale=x_scales[:, b, cols], start=(b == 0), stop=False)
-                    nc.tensor.matmul_mx(out=pair[:, 1, :], lhsT=w3_codes[:, b, rows].bitcast(FP8X4),
+                    nc.tensor.matmul_mx(out=both[:, QUARTER:HALF], lhsT=w3_codes[:, b, rows].bitcast(FP8X4),
                                         lhsT_scale=w3_scales[:, b, rows], rhs=x_codes[b][:, cols].bitcast(FP8X4),
+                                        rhs_scale=x_scales[:, b, cols], start=(b == 0), stop=False)
+                    nc.tensor.matmul_mx(out=both[:, 0:QUARTER], lhsT=w2_codes[:, b, 2 * u * P:2 * (u + 1) * P].bitcast(FP4X4),
+                                        lhsT_scale=w2_plane[:, b, rows], rhs=x_codes[b][:, cols].bitcast(FP8X4),
                                         rhs_scale=x_scales[:, b, cols], start=False, stop=(b == 1))
-                nc.scalar.activation(out=squares[:, u], in_=pair[:], func=ACT.Square)
-            total = sb.tile([P, N_TILES, QUARTER], F32, name="total%d" % q, tag="round", bufs=2, align_bytes=64)
-            nc.vector.tensor_tensor(out=total[:], in0=squares[:, :, 0, :], in1=squares[:, :, 1, :], op=ALU.add)
-            nc.scalar.activation(out=total[:], in_=total[:], func=ACT.Sqrt)
-            nc.sync.dma_start(out=y_rows[:, :, cols], in_=total[:])
+                nc.scalar.activation(out=squares[:, u].rearrange("p k m -> p (k m)"), in_=both[:], func=ACT.Square)
+            for lo, hi in steps:
+                nc.vector.tensor_tensor(out=total[:, lo:hi], in0=squares[:, lo:hi, 0, :], in1=squares[:, lo:hi, 1, :], op=ALU.add)
+                nc.scalar.activation(out=total[:, lo:hi], in_=total[:, lo:hi], func=ACT.Sqrt)
+                nc.sync.dma_start(out=y_rows[:, lo:hi, cols], in_=total[:, lo:hi])
 
         nc.vector.memset(tab_s[:].bitcast(I32), 0)
-        nc.vector.memset(w2_plane[:].rearrange("p b c -> p (b c)").bitcast(I32), 0)
+        make_identity(nc, ident[:])
+        for q in range(4):
+            nc.gpsimd.dma_start(out=tab_s[32 * q:32 * q + 8, :].bitcast(I32), in_=tab_scales[:, 4 * q:4 * q + 4, :].bitcast(I32))
+        nc.gpsimd.memset(w2_plane[:].rearrange("p b c -> p (b c)").bitcast(I32), 0)
 
         nc.sync.dma_start(out=idx[:], in_=offs)
+        wgs_rows = sb.tile([P, S], F32, name="wgs_rows", tag="h", bufs=2)
+        nc.sync.dma_start(out=wgs_rows[:], in_=wgs)
         tab_w = [big([P, T], I32, "tab_w%d" % a) for a in range(2)]
         nc.sync.dma_start(out=tab_w[0][:], in_=tab_words[0].rearrange("p n t -> p (n t)").bitcast(I32))
-        for q in range(4):
-            nc.sync.dma_start(out=tab_s[32 * q:32 * q + 8, :].bitcast(I32), in_=tab_scales[:, 4 * q:4 * q + 4, :].bitcast(I32))
         raw = [load_weight(w1[a * PASS:(a + 1) * PASS, 0:PASS], "w1_raw0%d" % a) for a in range(2)]
         nc.sync.dma_start(out=tab_w[1][:], in_=tab_words[1].rearrange("p n t -> p (n t)").bitcast(I32))
         floor_first = [sb.tile([P, HALF], F32, name="floor_first%d" % u, tag="floor", bufs=3) for u in range(2)]
         nc.sync.dma_start(out=floor_first[0][:], in_=tide_rows[0, 0][:, 0:HALF])
         nc.sync.dma_start(out=idx2[:], in_=offs2)
-        load_gain_first(0)
         pages = {0: load_page(0)}
         nc.sync.dma_start(out=floor_first[1][:], in_=tide_rows[0, 0][:, HALF:S])
-        load_gain_first(1)
         nc.sync.dma_start(out=idx3[:], in_=offs3)
         floors = {1: load_tide(1)}
-        for q in range(4):
-            nc.sync.dma_start(out=gain_rest[32 * q:32 * q + 32], in_=wgs_rows[:, 1:PACK, :])
-        pages[1] = load_page(1)
 
-        nc.vector.tensor_copy(out=v_codes[:, 0, :], in_=tab_w[0][:].bitcast(U32).indirect(idx[:]))
+        nc.vector.tensor_copy(out=v_codes[0][:], in_=tab_w[0][:].bitcast(U32).indirect(idx[:]))
         nc.vector.tensor_copy(out=v_scales[:], in_=tab_s[:].indirect(idx[:]))
-        quantise_w1(round_w1(raw[0], 0, 0, "scalar"), 0, 0)
-        quantise_w1(round_w1(raw[1], 0, 1, "vector"), 0, 1)
+        dealt = [turn_gain(wgs_rows, u) for u in range(2)]
         for u in range(2):
-            nc.vector.tensor_copy(out=v_codes[:, 1, u * HALF:(u + 1) * HALF],
+            deal_gain(dealt[u], 0, u)
+        quantise_w1(round_w1(raw[0], 0, 0, "vector"), 0, 0)
+        quantise_w1(round_w1(raw[1], 0, 1, "vector"), 0, 1)
+        for t in range(1, PACK):
+            for u in range(2):
+                deal_gain(dealt[u], t, u)
+        v_codes.append(sb.tile([P, S], U32, name="v_codes1", tag="tab_s", align_bytes=64))
+        for u in range(2):
+            nc.vector.tensor_copy(out=v_codes[1][:, u * HALF:(u + 1) * HALF],
                                   in_=tab_w[1][:].bitcast(U32).indirect(entries(idx, u * HALF, (u + 1) * HALF)))
 
         h = new_h(0)
         for u in range(2):
             features(0, u, floor_first[u][:], h)
-            put(pages[0], h, gain_first[u][:], u * HALF, (u + 1) * HALF)
+            put(0, pages[0], h, u * HALF, (u + 1) * HALF)
 
         raw = [load_weight(w1[a * PASS:(a + 1) * PASS, PASS:2 * PASS], "w1_raw1%d" % a) for a in range(2)]
         w1_round = [round_w1(raw[a], 1, a, "scalar") for a in range(2)]
+        pages[1] = load_page(1)
+        floors[2] = load_tide(2)
 
         last = TILES - 1
         picked = pairs = woven = woven_last = planes = w3_round = w3_codes = None
@@ -220,8 +236,9 @@ def tile_list_nest_board_risk_kernel(tc, tab_words, tab_scales, offs, w1, tide, 
             b, t = divmod(i, PACK)
             pair, e = divmod(t, 2)
             if i + 2 < TILES:
-                floors[i + 2] = load_tide(i + 2)
                 pages[i + 2] = load_page(i + 2)
+            if i + 3 < TILES:
+                floors[i + 3] = load_tide(i + 3)
             nc.sync.dma_start(out=out_rows[b, t], in_=pages[i][:])
             if i == last:
                 break
@@ -240,9 +257,6 @@ def tile_list_nest_board_risk_kernel(tc, tab_words, tab_scales, offs, w1, tide, 
             else:
                 nc.scalar.copy(out=planes[:, 0, :], in_=pages[i][:])
             if i == 2:
-                w1_codes[1] = after(2, [P, 2, PASS], U32, "w1_codes1")
-                for a in range(2):
-                    quantise_w1(w1_round[a], 1, a)
                 nc.sync.dma_start(out=w2_codes[:].bitcast(I32), in_=w2_words.rearrange("b p c -> p b c").bitcast(I32))
                 for q in range(4):
                     nc.sync.dma_start(out=w2_plane[32 * q:32 * q + 4].bitcast(I32),
@@ -254,6 +268,10 @@ def tile_list_nest_board_risk_kernel(tc, tab_words, tab_scales, offs, w1, tide, 
             fetch(pages[i], picked, e, 0, PICK)
             if e == 1:
                 round_x(picked, pair, 0, PICK)
+            if i == 2:
+                w1_codes[1] = after(2, [P, 2, PASS], U32, "w1_codes1")
+                for a in range(2):
+                    quantise_w1(w1_round[a], 1, a)
             if i == 3:
                 woven = big([P, T2, PACK], BF16, "woven0")
                 nc.scalar.copy(out=woven[:].rearrange("p m t -> p (m t)").bitcast(U32).rearrange("p (m h) -> p m h", h=2),
@@ -272,7 +290,7 @@ def tile_list_nest_board_risk_kernel(tc, tab_words, tab_scales, offs, w1, tide, 
                 w3_codes = after(6, [P, 2, N], U32, "w3_codes")
                 for a in range(2):
                     nc.vector.quantize_mx(out=w3_codes[:, a, :].bitcast(FP8X4), scales=w3_scales[:, a, :], in_=w3_round[a][:])
-            put_tile(i + 1, pages[i + 1], h)
+            put(i + 1, pages[i + 1], h, 0, S)
 
         codes = sb.tile([P, T2], U32, name="codes1", align_bytes=64)
         scales = sb.tile([P, T2], U8, name="scales1", align_bytes=64)
@@ -283,10 +301,9 @@ def tile_list_nest_board_risk_kernel(tc, tab_words, tab_scales, offs, w1, tide, 
             quantise_x(1, q * QUARTER, (q + 1) * QUARTER)
         for q in range(4):
             lo, hi = q * HALF, (q + 1) * HALF
-            score(q, w3_codes)
-            nc.vector.tensor_copy(out=planes[:, 1, lo:hi], in_=pages[last][:, lo:hi])
+            score(q, w3_codes, [(0, N_TILES)] if q < 3 else [(0, N_TILES - 1), (N_TILES - 1, N_TILES)])
+            copy_on("scalar" if q == 0 else "vector", planes[:, 1, lo:hi], pages[last][:, lo:hi])
             nc.vector.tensor_copy(out=woven_last[:, lo:hi, 2:4], in_=planes[:, :, lo:hi].rearrange("p e m -> p m e"))
             quantise_page(woven_last, codes, scales, lo, hi)
-            if q % 2 == 1:
-                store_codes(1, codes, lo - HALF, hi)
+            store_codes(1, codes, lo, hi)
         store_scales(1, scales)

@@ -186,6 +186,9 @@ def tile_list_nest_board_risk_kernel(tc, tab_words, tab_scales, offs, w1, tide, 
 
         nc.vector.memset(tab_s[:].bitcast(I32), 0)
         make_identity(nc, ident[:])
+        warm = sb.tile([P, 1], F32, name="warm")
+        nc.gpsimd.memset(warm[:], 1.0)
+        nc.scalar.activation(out=warm[:], in_=warm[:], func=ACT.Sqrt)
         for q in range(4):
             nc.gpsimd.dma_start(out=tab_s[32 * q:32 * q + 8, :].bitcast(I32), in_=tab_scales[:, 4 * q:4 * q + 4, :].bitcast(I32))
         nc.gpsimd.memset(w2_plane[:].rearrange("p b c -> p (b c)").bitcast(I32), 0)

from contextlib import ExitStack

import concourse.mybir as mybir
from concourse.masks import make_identity

K, T, S, H, T2, PICK, N = 1024, 4096, 1024, 1024, 2048, 1024, 384
FLOPS = 2 * K * H * S + 2 * 2 * H * N * PICK

F32 = mybir.dt.float32
BF16 = mybir.dt.bfloat16
I32 = mybir.dt.int32
U32 = mybir.dt.uint32
U16 = mybir.dt.uint16
U8 = mybir.dt.uint8
FP8X4 = mybir.dt.float8_e4m3fn_x4
FP4X4 = mybir.dt.float4_e2m1fn_x4
ALU = mybir.AluOpType
ACT = mybir.ActivationFunctionType

P = 128
PACK = 4
PASS = P * PACK
HALF = 512
QUARTER = 256
LANES = 16
TILES = H // P
N_TILES = N // P
HELD = (2, 4, 5, 6)


def tile_list_nest_board_risk_kernel(tc, tab_words, tab_scales, offs, w1, tide, page0, wgs, offs2, offs3,
                                              w2_words, w2_scales, w3, out_0, out_1, out_2, out_3):
    nc = tc.nc
    tide_rows = tide.rearrange("(b p t) j -> b t p j", p=P, t=PACK)
    page_rows = page0.rearrange("(b p t) m -> b t p m", p=P, t=PACK)
    out_rows = out_1.rearrange("(b p t) m -> b t p m", p=P, t=PACK)
    y_rows = out_0.rearrange("(u p) m -> p u m", p=P)

    with ExitStack() as ctx:
        sb = ctx.enter_context(tc.tile_pool(name="sb", bufs=1))
        ps = ctx.enter_context(tc.psum_pool(name="ps", bufs=8))

        idx = sb.tile([P, S // LANES], U16, name="idx")
        idx2 = sb.tile([P, S // LANES], U16, name="idx2")
        idx3 = sb.tile([P, PICK // LANES], U16, name="idx3")
        tab_s = sb.tile([P, T], U8, name="tab_s", tag="tab_s", align_bytes=64)
        v_codes = [sb.tile([P, S], U32, name="v_codes0", align_bytes=64)]
        v_scales = sb.tile([P, S], U8, name="v_scales", align_bytes=64)
        w1_codes = {0: sb.tile([P, 2, PASS], U32, name="w1_codes0", align_bytes=64)}
        w1_scales = sb.tile([P, 2, 2, PASS], U8, name="w1_scales", align_bytes=64)
        w2_codes = sb.tile([P, 2, 2 * N], U8, name="w2_codes", align_bytes=64)
        w2_plane = sb.tile([P, 2, N], U8, name="w2_plane", align_bytes=64)
        w3_scales = sb.tile([P, 2, N], U8, name="w3_scales", align_bytes=64)
        x_codes = {1: sb.tile([P, PICK], U32, name="x_codes1", align_bytes=64)}
        x_scales = sb.tile([P, 2, PICK], U8, name="x_scales", align_bytes=64)
        x_round = sb.tile([P, PICK, PACK], BF16, name="x_round", align_bytes=64)
        gain = sb.tile([P, PACK, S], F32, name="gain")
        ident = sb.tile([P, P], F32, name="ident")

        def big(shape, dtype, name):
            return sb.tile(shape, dtype, name=name, tag="big", bufs=2, align_bytes=64)

        def entries(lst, lo, hi):
            return lst[:, lo // LANES: hi // LANES]

        def load_weight(rows, name):
            raw = sb.tile([P, PACK, rows.shape[1]], F32, name=name, tag="raw", bufs=2)
            nc.sync.dma_start(out=raw[:], in_=rows.rearrange("(p j) c -> p j c", j=PACK))
            return raw

        def copy_on(engine, out, in_):
            if engine == "vector":
                nc.vector.tensor_copy(out=out, in_=in_)
            else:
                nc.scalar.copy(out=out, in_=in_)

        def after(i, shape, dtype, name):
            return sb.tile(shape, dtype, name=name, tag="after%d" % i, align_bytes=64)

        def new_h(i):
            if i in HELD:
                return after(i, [P, S], F32, "h%d" % i)
            return sb.tile([P, S], F32, name="h%d" % i, tag="h", bufs=2)

        def round_w1(raw, b, a, engine):
            rounded = sb.tile([P, PACK * PASS], BF16, name="w1_round%d%d" % (b, a), tag="round", bufs=2, align_bytes=64)
            copy_on(engine, rounded[:].rearrange("p (t m j) -> p m j t", t=PACK, j=PACK),
                    raw[:].rearrange("p j (m t) -> p m j t", t=PACK))
            return rounded

        def quantise_w1(rounded, b, a):
            nc.vector.quantize_mx(out=w1_codes[b][:, a, :].bitcast(FP8X4), scales=w1_scales[:, b, a, :], in_=rounded[:])

        def round_w3(raw, a):
            rounded = sb.tile([P, PACK * N], BF16, name="w3_round%d" % a, tag="round", bufs=2, align_bytes=64)
            nc.scalar.copy(out=rounded[:].rearrange("p (c i j) -> p c j i", i=4, j=PACK),
                           in_=raw[:].rearrange("p j (c i) -> p c j i", i=4))
            return rounded

        def load_page(i):
            page = sb.tile([P, T2], F32, name="page%d" % i, tag="page", bufs=4)
            nc.sync.dma_start(out=page[:], in_=page_rows[i // PACK, i % PACK])
            return page

        def load_tide(i):
            floor = sb.tile([P, S], F32, name="floor%d" % i, tag="floor", bufs=3)
            nc.sync.dma_start(out=floor[:], in_=tide_rows[i // PACK, i % PACK])
            return floor

        def bank(name):
            return ps.tile([P, HALF], F32, name=name, tag="bank")

        def turn_gain(rows, u):
            turned = bank("turned%d" % u)
            for c in range(4):
                col = u * HALF + c * P
                nc.tensor.transpose(turned[:, c * P:(c + 1) * P], rows[:, col:col + P], ident[:])
            dealt = sb.tile([P, 4, PACK, 4, 32], F32, name="dealt%d" % u, tag="picked", bufs=2)
            nc.scalar.copy(out=dealt[:], in_=turned[:].rearrange("p (c i t) -> p c t i", c=4, t=PACK).unsqueeze(3)
                           .broadcast_to([P, 4, PACK, 4, 32]))
            return dealt

        def deal_gain(dealt, t, u):
            back = bank("back%d%d" % (t, u))
            for c in range(4):
                nc.tensor.transpose(back[:, c * P:(c + 1) * P], dealt[:, c, t].rearrange("p q i -> p (q i)"), ident[:])
            nc.scalar.copy(out=gain[:, t, u * HALF:(u + 1) * HALF], in_=back[:])

        def features(i, u, floor_half, h):
            b, t = divmod(i, PACK)
            cols = slice(u * HALF, (u + 1) * HALF)
            rows = slice(t * P, (t + 1) * P)
            acc = bank("acc%d%d" % (i, u))
            for a in range(2):
                nc.tensor.matmul_mx(out=acc[:], lhsT=w1_codes[b][:, a, rows].bitcast(FP8X4), lhsT_scale=w1_scales[:, b, a, rows],
                                    rhs=v_codes[a][:, cols].bitcast(FP8X4), rhs_scale=v_scales[4 * a:P, cols],
                                    start=(a == 0), stop=(a == 1))
            nc.vector.tensor_tensor(out=h[:, cols], in0=acc[:], in1=floor_half, op=ALU.max)

        def put(i, page, h, lo, hi):
            nc.vector.tensor_tensor(out=page[:].indirect(entries(idx2, lo, hi)), in0=h[:, lo:hi],
                                    in1=gain[:, i % PACK, lo:hi], op=ALU.mult)

        def fetch(page, picked, e, lo, hi):
            nc.vector.tensor_copy(out=picked[:, e, lo:hi], in_=page[:].indirect(entries(idx3, lo, hi)))

        def round_x(picked, pair, lo, hi):
            nc.scalar.activation(out=x_round[:, lo:hi, 2 * pair:2 * pair + 2],
                                 in_=picked[:, :, lo:hi].rearrange("p e m -> p m e"), func=ACT.Abs)

        def quantise_x(b, lo, hi):
            nc.vector.quantize_mx(out=x_codes[b][:, lo:hi].bitcast(FP8X4), scales=x_scales[:, b, lo:hi],
                                  in_=x_round[:, lo:hi, :].rearrange("p m t -> p (m t)"))

        def quantise_page(woven, codes, scales, lo, hi):
            nc.vector.quantize_mx(out=codes[:, lo:hi].bitcast(FP8X4), scales=scales[:, lo:hi],
                                  in_=woven[:, lo:hi, :].rearrange("p m t -> p (m t)"))

        def store_codes(b, codes, lo, hi):
            words = out_2[b].rearrange("p m t -> p (m t)").bitcast(I32)
            nc.sync.dma_start(out=words[:, lo:hi], in_=codes[:, lo:hi].bitcast(I32))

        def store_scales(b, scales):
            for q in range(4):
                nc.sync.dma_start(out=out_3[b, 4 * q:4 * q + 4, :].bitcast(I32), in_=scales[32 * q:32 * q + 4, :].bitcast(I32))

        def score(q, w3_codes, steps):
            cols = slice(q * QUARTER, (q + 1) * QUARTER)
            squares = sb.tile([P, N_TILES, 2, QUARTER], F32, name="squares%d" % q, tag="raw", bufs=2)
            total = sb.tile([P, N_TILES, QUARTER], F32, name="total%d" % q, tag="round", bufs=2, align_bytes=64)
            for u in range(N_TILES):
                both = bank("both%d%d" % (q, u))
                rows = slice(u * P, (u + 1) * P)
                for b in range(2):
                    nc.tensor.matmul_mx(out=both[:, QUARTER:HALF], lhsT=w3_codes[:, b, rows].bitcast(FP8X4),
                                        lhsT_scale=w3_scales[:, b, rows], rhs=x_codes[b][:, cols].bitcast(FP8X4),
                                        rhs_scale=x_scales[:, b, cols], start=(b == 0), stop=False)
                    nc.tensor.matmul_mx(out=both[:, 0:QUARTER], lhsT=w2_codes[:, b, 2 * u * P:2 * (u + 1) * P].bitcast(FP4X4),
                                        lhsT_scale=w2_plane[:, b, rows], rhs=x_codes[b][:, cols].bitcast(FP8X4),
                                        rhs_scale=x_scales[:, b, cols], start=False, stop=(b == 1))
                nc.scalar.activation(out=squares[:, u].rearrange("p k m -> p (k m)"), in_=both[:], func=ACT.Square)
            for lo, hi in steps:
                nc.vector.tensor_tensor(out=total[:, lo:hi], in0=squares[:, lo:hi, 0, :], in1=squares[:, lo:hi, 1, :], op=ALU.add)
                nc.scalar.activation(out=total[:, lo:hi], in_=total[:, lo:hi], func=ACT.Sqrt)
                nc.sync.dma_start(out=y_rows[:, lo:hi, cols], in_=total[:, lo:hi])

        nc.vector.memset(tab_s[:].bitcast(I32), 0)
        make_identity(nc, ident[:])
        warm = sb.tile([P, 1], F32, name="warm")
        nc.gpsimd.memset(warm[:], 1.0)
        nc.scalar.activation(out=warm[:], in_=warm[:], func=ACT.Sqrt)
        for q in range(4):
            nc.gpsimd.dma_start(out=tab_s[32 * q:32 * q + 8, :].bitcast(I32), in_=tab_scales[:, 4 * q:4 * q + 4, :].bitcast(I32))
        nc.gpsimd.memset(w2_plane[:].rearrange("p b c -> p (b c)").bitcast(I32), 0)

        nc.sync.dma_start(out=idx[:], in_=offs)
        wgs_rows = sb.tile([P, S], F32, name="wgs_rows", tag="h", bufs=2)
        nc.sync.dma_start(out=wgs_rows[:], in_=wgs)
        tab_w = [big([P, T], I32, "tab_w%d" % a) for a in range(2)]
        nc.sync.dma_start(out=tab_w[0][:], in_=tab_words[0].rearrange("p n t -> p (n t)").bitcast(I32))
        raw = [load_weight(w1[a * PASS:(a + 1) * PASS, 0:PASS], "w1_raw0%d" % a) for a in range(2)]
        nc.sync.dma_start(out=tab_w[1][:], in_=tab_words[1].rearrange("p n t -> p (n t)").bitcast(I32))
        floor_first = [sb.tile([P, HALF], F32, name="floor_first%d" % u, tag="floor", bufs=3) for u in range(2)]
        nc.sync.dma_start(out=floor_first[0][:], in_=tide_rows[0, 0][:, 0:HALF])
        nc.sync.dma_start(out=idx2[:], in_=offs2)
        pages = {0: load_page(0)}
        nc.sync.dma_start(out=floor_first[1][:], in_=tide_rows[0, 0][:, HALF:S])
        nc.sync.dma_start(out=idx3[:], in_=offs3)
        floors = {1: load_tide(1)}

        nc.vector.tensor_copy(out=v_codes[0][:], in_=tab_w[0][:].bitcast(U32).indirect(idx[:]))
        nc.vector.tensor_copy(out=v_scales[:], in_=tab_s[:].indirect(idx[:]))
        dealt = [turn_gain(wgs_rows, u) for u in range(2)]
        for u in range(2):
            deal_gain(dealt[u], 0, u)
        quantise_w1(round_w1(raw[0], 0, 0, "vector"), 0, 0)
        quantise_w1(round_w1(raw[1], 0, 1, "vector"), 0, 1)
        for t in range(1, PACK):
            for u in range(2):
                deal_gain(dealt[u], t, u)
        v_codes.append(sb.tile([P, S], U32, name="v_codes1", tag="tab_s", align_bytes=64))
        for u in range(2):
            nc.vector.tensor_copy(out=v_codes[1][:, u * HALF:(u + 1) * HALF],
                                  in_=tab_w[1][:].bitcast(U32).indirect(entries(idx, u * HALF, (u + 1) * HALF)))

        h = new_h(0)
        for u in range(2):
            features(0, u, floor_first[u][:], h)
            put(0, pages[0], h, u * HALF, (u + 1) * HALF)

        raw = [load_weight(w1[a * PASS:(a + 1) * PASS, PASS:2 * PASS], "w1_raw1%d" % a) for a in range(2)]
        w1_round = [round_w1(raw[a], 1, a, "scalar") for a in range(2)]
        pages[1] = load_page(1)
        floors[2] = load_tide(2)

        last = TILES - 1
        picked = pairs = woven = woven_last = planes = w3_round = w3_codes = None
        for i in range(TILES):
            b, t = divmod(i, PACK)
            pair, e = divmod(t, 2)
            if i + 2 < TILES:
                pages[i + 2] = load_page(i + 2)
            if i + 3 < TILES:
                floors[i + 3] = load_tide(i + 3)
            nc.sync.dma_start(out=out_rows[b, t], in_=pages[i][:])
            if i == last:
                break
            if e == 0:
                picked = sb.tile([P, 2, PICK], F32, name="picked%d" % i, tag="picked", bufs=2)
            if i == 0:
                pairs = big([P, 2, T2, 2], BF16, "pairs")
            if i == 4:
                woven_last = big([P, T2, PACK], BF16, "woven1")
            if i == 6:
                planes = big([P, 2, T2], BF16, "planes")
            if b == 0:
                nc.scalar.copy(out=pairs[:, pair, :, e], in_=pages[i][:])
            elif pair == 0:
                nc.scalar.copy(out=woven_last[:, :, t], in_=pages[i][:])
            else:
                nc.scalar.copy(out=planes[:, 0, :], in_=pages[i][:])
            if i == 2:
                nc.sync.dma_start(out=w2_codes[:].bitcast(I32), in_=w2_words.rearrange("b p c -> p b c").bitcast(I32))
                for q in range(4):
                    nc.sync.dma_start(out=w2_plane[32 * q:32 * q + 4].bitcast(I32),
                                      in_=w2_scales[:, 4 * q:4 * q + 4, :].rearrange("b r c -> r b c").bitcast(I32))
                w3_round = [round_w3(load_weight(w3[a * PASS:(a + 1) * PASS, :], "w3_raw%d" % a), a) for a in range(2)]
            h = new_h(i + 1)
            for u in range(2):
                features(i + 1, u, floors[i + 1][:, u * HALF:(u + 1) * HALF], h)
            fetch(pages[i], picked, e, 0, PICK)
            if e == 1:
                round_x(picked, pair, 0, PICK)
            if i == 2:
                w1_codes[1] = after(2, [P, 2, PASS], U32, "w1_codes1")
                for a in range(2):
                    quantise_w1(w1_round[a], 1, a)
            if i == 3:
                woven = big([P, T2, PACK], BF16, "woven0")
                nc.scalar.copy(out=woven[:].rearrange("p m t -> p (m t)").bitcast(U32).rearrange("p (m h) -> p m h", h=2),
                               in_=pairs[:].rearrange("p h m e -> p (h m e)").bitcast(U32).rearrange("p (h m) -> p m h", h=2))
            if i == 4:
                x_codes[0] = after(4, [P, PICK], U32, "x_codes0")
                quantise_x(0, 0, PICK)
            if i == 5:
                codes = after(5, [P, T2], U32, "codes0")
                scales = sb.tile([P, T2], U8, name="scales0", align_bytes=64)
                for u in range(2):
                    quantise_page(woven, codes, scales, u * T2 // 2, (u + 1) * T2 // 2)
                store_codes(0, codes, 0, T2)
                store_scales(0, scales)
            if i == 6:
                w3_codes = after(6, [P, 2, N], U32, "w3_codes")
                for a in range(2):
                    nc.vector.quantize_mx(out=w3_codes[:, a, :].bitcast(FP8X4), scales=w3_scales[:, a, :], in_=w3_round[a][:])
            put(i + 1, pages[i + 1], h, 0, S)

        codes = sb.tile([P, T2], U32, name="codes1", align_bytes=64)
        scales = sb.tile([P, T2], U8, name="scales1", align_bytes=64)
        for q in range(4):
            fetch(pages[last], picked, 1, q * QUARTER, (q + 1) * QUARTER)
            round_x(picked, 1, q * QUARTER, (q + 1) * QUARTER)
        for q in range(4):
            quantise_x(1, q * QUARTER, (q + 1) * QUARTER)
        for q in range(4):
            lo, hi = q * HALF, (q + 1) * HALF
            score(q, w3_codes, [(0, N_TILES)] if q < 3 else [(0, N_TILES - 1), (N_TILES - 1, N_TILES)])
            copy_on("scalar" if q == 0 else "vector", planes[:, 1, lo:hi], pages[last][:, lo:hi])
            nc.vector.tensor_copy(out=woven_last[:, lo:hi, 2:4], in_=planes[:, :, lo:hi].rearrange("p e m -> p m e"))
            quantise_page(woven_last, codes, scales, lo, hi)
            store_codes(1, codes, lo, hi)
        store_scales(1, scales)
